import numpy as np
import ml_dtypes


def mxq(x, axis, fmt="e4m3"):
    dtype, down = {"e4m3": (ml_dtypes.float8_e4m3fn, 7), "e5m2": (ml_dtypes.float8_e5m2, 14)}[fmt]
    v = np.moveaxis(np.asarray(x, np.float32).astype(ml_dtypes.bfloat16).astype(np.float64), axis, -1)
    blocks = v.reshape(v.shape[:-1] + (-1, 32))
    amax = np.abs(blocks).max(-1, keepdims=True)
    byte = np.maximum(np.where(amax > 0, np.frexp(amax)[1] - 1 + 127, 0) - down, 1)
    scale = np.exp2(byte - 127.0)
    codes = (blocks / scale).astype(np.float32).astype(dtype).astype(np.float64)
    return np.moveaxis((codes * scale).reshape(v.shape), -1, axis)


WIDE = False


def mx_kscale(k):
    if not WIDE:
        return np.ones(k)
    levels = np.array([10, -10, 5, -5, 0])
    if k % 512:
        return np.exp2(np.random.permutation(np.resize(levels, k // 32))).repeat(32)
    a = np.empty((k // 512, 16))
    for p in range(k // 512):
        a[p, :8] = np.random.permutation(np.resize(levels, 8))
        for g in range(8):
            far = levels[np.abs(levels - a[p, g]) >= 10]
            a[p, g + 8] = far[np.random.randint(len(far))]
    return np.exp2(a.ravel()).repeat(32)


def f64(x):
    return np.asarray(x).astype(np.float64)


def striped(idx):
    return np.tile(idx.reshape(-1, 16).T, (8, 1)).astype(np.uint16)


def unstriped(offs):
    return offs[:16].T.reshape(-1).astype(np.int64)


E2M1 = np.array([0.0, 0.5, 1.0, 1.5, 2.0, 3.0, 4.0, 6.0, -0.0, -0.5, -1.0, -1.5, -2.0, -3.0, -4.0, -6.0])


def pack_weight(w, fmt):
    k, n = w.shape
    w = f64(np.asarray(w, np.float32).astype(ml_dtypes.bfloat16)).reshape(k // 32, 32, n)
    amax = np.abs(w).max(1)
    if fmt == "e4m3":
        byte = np.frexp(amax)[1] - 1 + 127 - 7
    else:
        mant, ex = np.frexp(amax / 6.0)
        byte = np.where(mant > 0.5, ex, ex - 1) + 127
    byte = np.clip(np.where(amax > 0, byte, 1), 1, 254)
    scaled = (w * np.exp2(127.0 - byte)[:, None, :]).reshape(k, n).astype(np.float32)
    by_word = np.ascontiguousarray(scaled.reshape(k // 512, 128, 4, n).transpose(0, 1, 3, 2))
    if fmt == "e4m3":
        words = by_word.astype(ml_dtypes.float8_e4m3fn).view(np.uint8)
    else:
        c = by_word.astype(ml_dtypes.float4_e2m1fn).view(np.uint8) & 0xF
        words = (c[..., 0::2] | (c[..., 1::2] << 4)).reshape(k // 512, 128, 2 * n)
    return np.ascontiguousarray(words), np.ascontiguousarray(byte.astype(np.uint8).reshape(k // 512, 16, n))


def unpack_weight(words, scales, fmt):
    g, _, n = scales.shape
    words = np.ascontiguousarray(words).reshape(g, 128, n, -1)
    if fmt == "e4m3":
        vals = words.view(ml_dtypes.float8_e4m3fn).astype(np.float64)
    else:
        nib = np.empty((g, 128, n, 4), np.uint8)
        nib[..., 0::2] = words & 0xF
        nib[..., 1::2] = words >> 4
        vals = E2M1[nib]
    vals = vals * np.repeat(np.exp2(scales.astype(np.float64) - 127.0), 8, axis=1)[..., None]
    return vals.transpose(0, 1, 3, 2).reshape(g * 512, n)


def gelu(v):
    return 0.5 * v * (1.0 + np.tanh(np.sqrt(2.0 / np.pi) * (v + 0.044715 * v**3)))


def bf(x):
    return np.asarray(x, np.float32).astype(ml_dtypes.bfloat16)


def planes(Y):
    n, m = Y.shape
    b = f64(bf(Y)).reshape(n // 32, 32, m)
    amax = np.abs(b).max(1)
    byte = np.clip(np.where(amax > 0, np.frexp(amax)[1] - 1 + 127 - 7, 1), 1, 254)
    codes = (b * np.exp2(127.0 - byte)[:, None, :]).reshape(n, m).astype(np.float32).astype(ml_dtypes.float8_e4m3fn).view(np.uint8)
    words = codes.reshape(n // 512, 128, 4, m).transpose(0, 1, 3, 2)
    return np.ascontiguousarray(words), np.ascontiguousarray(byte.astype(np.uint8).reshape(n // 512, 16, m))


K, M, H, N, T, S, T2, P = 1024, 512, 1024, 512, 2048, 1024, 2048, 1024

def setup_inputs():
    n = np.random.standard_normal
    s = mx_kscale(K)[:, None]
    q = mx_kscale(M)[:, None]
    u = mx_kscale(H)[:, None]
    d = {}
    d["tab_words"], d["tab_scales"] = pack_weight(n((K, T)) * s, "e4m3")
    d["offs"] = striped(np.random.permutation(T)[:S])
    d["offs2"] = striped(np.random.permutation(T2)[:S])
    d["offs3"] = striped(np.random.permutation(T2)[:P])
    d["w1"] = (1.8 * n((K, M)) / K ** 0.5 / s).astype(np.float32)
    d["gain"] = (np.exp(0.3 * n(M)) * q[:, 0]).astype(np.float32)
    d["w2_words"], d["w2_scales"] = pack_weight(n((M, H)) / M ** 0.5 / q * u.T, "e2m1")
    d["w3"] = (0.8 * n((K, H)) / K ** 0.5 / s * u.T).astype(np.float32)
    d["wgs"] = np.exp(0.3 * n((128, S))).astype(np.float32)
    d["page0"] = (1.2 * n((H, T2)) * u).astype(np.float32)
    d["rain"] = (n((H, P)) * u).astype(np.float32)
    d["w4_words"], d["w4_scales"] = pack_weight(n((H, N)) / H ** 0.5 / u, "e4m3")
    d["by"] = (0.8 * n(N)).astype(np.float32)
    return d

def reference(tab_words, tab_scales, offs, offs2, offs3, w1, gain, w2_words, w2_scales, w3, wgs, page0, rain, w4_words, w4_scales, by):
    v = unpack_weight(tab_words, tab_scales, "e4m3")[:, unstriped(offs)]
    a = mxq(f64(w1), 0, "e4m3").T @ v
    f = a / (1.0 + np.exp(-a)) * f64(gain)[:, None]
    w2 = unpack_weight(w2_words, w2_scales, "e2m1")
    h = w2.T @ mxq(f, 0, "e4m3") + mxq(f64(w3), 0, "e4m3").T @ v
    page = f64(page0).copy()
    page[:, unstriped(offs2)] = np.tile(f64(wgs), (H // 128, 1)) * h
    x = page[:, unstriped(offs3)] - f64(rain)
    w4 = unpack_weight(w4_words, w4_scales, "e4m3")
    y = (w4.T @ mxq(x, 0, "e4m3")) + f64(by)[:, None]
    words, scales = planes(page)
    return y, page, words, scales

@@ -1,0 +1,353 @@
+from contextlib import ExitStack
+
+import concourse.mybir as mybir
+
+K, M, H, N, T, S, T2, PX = 1024, 512, 1024, 512, 2048, 1024, 2048, 1024
+FLOPS = 2 * S * (K * M + M * H + K * H) + 2 * PX * H * N
+
+F32 = mybir.dt.float32
+BF16 = mybir.dt.bfloat16
+I32 = mybir.dt.int32
+U32 = mybir.dt.uint32
+U16 = mybir.dt.uint16
+U8 = mybir.dt.uint8
+E4M3 = mybir.dt.float8_e4m3fn_x4
+E2M1 = mybir.dt.float4_e2m1fn_x4
+ACT = mybir.ActivationFunctionType
+ALU = mybir.AluOpType
+P = 128
+HALF = 512
+
+
+def tile_list_tapping_panel_board_kernel(tc, tab_words, tab_scales, offs, offs2, offs3, w1, gain, w2_words,
+                                                  w2_scales, w3, wgs, page0, rain, w4_words, w4_scales, by,
+                                                  out_0, out_1, out_2, out_3):
+    nc = tc.nc
+    with ExitStack() as ctx:
+        keep = ctx.enter_context(tc.tile_pool(name="keep", bufs=1))
+        psum = ctx.enter_context(tc.psum_pool(name="psum", bufs=8))
+
+        def held(name, cols, dtype, tag=None):
+            return keep.tile([P, cols], dtype, name=name, tag=tag or name, align_bytes=64)
+
+        idx = keep.tile([P, S // 16], U16, name="idx")
+        idx2 = keep.tile([P, S // 16], U16, name="idx2")
+        idx3 = keep.tile([P, PX // 16], U16, name="idx3")
+        tab_w = [held(f"tab_w{a}", T, U32) for a in range(2)]
+        tab_s = held("tab_s", T, U8)
+        tab_rows = held("tab_rows", T, U8)
+        v_w = [[held(f"v_w{a}{h}", HALF, U32) for h in range(2 - a)] for a in range(2)]
+        rounded = [held(f"rounded{i}", 2048, BF16) for i in range(3)]
+        v_s = held("v_s", S, U8)
+        pair = held("pair", 4096, F32)
+        raw_a = [pair[:, 2048 * a: 2048 * (a + 1)] for a in range(2)]
+        raw_b = [held(f"raw_b{a}", 2048, F32) for a in range(2)]
+        w1_w = [held(f"w1_w{a}", HALF, U32) for a in range(2)]
+        w1_s = [held(f"w1_s{a}", HALF, U8) for a in range(2)]
+        w3_w = [[held(f"w3_w{g}{a}", HALF, U32) for a in range(2)] for g in range(2)]
+        w3_s = [[held(f"w3_s{g}{a}", HALF, U8) for a in range(2)] for g in range(2)]
+        w2_raw = held("w2_raw", 2 * H, U8)
+        w2_w = held("w2_w", 2 * H, U8)
+        w2_sraw = held("w2_sraw", H, U8)
+        w2_s = held("w2_s", H, U8)
+        w4_w = [held(f"w4_w{g}", N, U32) for g in range(2)]
+        w4_s = held("w4_s", N, U8)
+        wg = [held(f"wg{u}", 2 * S, F32) for u in range(2)]
+        pages = [held(f"page{s}", T2, F32) for s in range(8)]
+        wide = held("wide", 4096, F32)
+        f_w = [held(f"f_w{h}", HALF, U32) for h in range(2)]
+        f_s = [held(f"f_s{h}", HALF, U8) for h in range(2)]
+        xs = [held(f"xs{i}", 2048, F32) for i in range(2)]
+        pg_w = [held("pg_w0", T2, U32)]
+        pg_s = [held(f"pg_s{g}", T2, U8) for g in range(2)]
+        x_w = [held(f"x_w{g}", PX, U32) for g in range(2)]
+        x_s = [held(f"x_s{g}", PX, U8) for g in range(2)]
+        gain_t = held("gain_t", 4, F32)
+        by_t = held("by_t", 4, F32)
+        warm = held("warm", 2, F32)
+
+        def page_rows(ap, s):
+            g, t = divmod(s, 4)
+            return ap[512 * g: 512 * (g + 1), :].rearrange("(p t) c -> p t c", t=4)[:, t, :]
+
+        def load_words(dst, src):
+            nc.sync.dma_start(out=dst[:].bitcast(I32), in_=src.rearrange("p n i -> p (n i)").bitcast(I32))
+
+        def load_rows(dst, src):
+            nc.sync.dma_start(out=dst.rearrange("p (j c) -> p j c", j=4), in_=src.rearrange("(p j) c -> p j c", j=4))
+
+        def load_planes(dst, src):
+            passes = src.shape[0]
+            for q in range(4):
+                nc.sync.dma_start(out=dst[32 * q: 32 * q + 4 * passes, :].bitcast(I32),
+                                    in_=src[:, 4 * q: 4 * q + 4, :].bitcast(I32))
+
+        def load_wg(t0, t1):
+            rows = wgs.rearrange("(q t) j -> q (t j)", t=4)[:, t0 * S: t1 * S]
+            for q in range(4):
+                nc.sync.dma_start(out=wg[t0 // 2][32 * q: 32 * (q + 1), (t0 % 2) * S: (t0 % 2 + t1 - t0) * S], in_=rows)
+
+        nc.vector.memset(warm[:], 0.0)
+        nc.scalar.activation(warm[:, 1:2], warm[:, 0:1], ACT.Silu)
+
+        for plane in (tab_s, w2_sraw, w4_s):
+            nc.vector.memset(plane[:].bitcast(U32), 0)
+
+        def load_page(s):
+            nc.sync.dma_start(out=pages[s][:], in_=page_rows(page0, s))
+
+        nc.sync.dma_start(idx[:], offs)
+        load_planes(tab_rows, tab_scales)
+        load_rows(raw_a[0][:], w1[0:512, :])
+        load_words(tab_w[0], tab_words[0])
+        nc.sync.dma_start(out=w2_raw[:].bitcast(I32), in_=w2_words[0].bitcast(I32))
+        load_rows(raw_a[1][:], w1[512:1024, :])
+        load_words(tab_w[1], tab_words[1])
+        nc.sync.dma_start(out=gain_t[:], in_=gain.rearrange("(p t) -> p t", t=4))
+        load_rows(raw_b[0][:], w3[0:512, 0:512])
+        load_rows(raw_b[1][:], w3[512:1024, 0:512])
+        load_planes(w2_sraw, w2_scales)
+        load_wg(0, 1)
+        load_page(0)
+        nc.sync.dma_start(idx2[:], offs2)
+        load_wg(1, 2)
+        load_page(1)
+
+        def deal_round(raw, on_vector, wb):
+            dst = wb[:].rearrange("p (t m j) -> p m j t", t=4, j=4)
+            src = raw[:].rearrange("p (j m t) -> p m j t", j=4, t=4)
+            if on_vector:
+                nc.vector.tensor_copy(out=dst, in_=src)
+            else:
+                nc.scalar.copy(out=dst, in_=src)
+            return wb
+
+        def quantize(words, scales, src):
+            nc.vector.quantize_mx(out=words.bitcast(E4M3), scales=scales, in_=src)
+
+        def gather_table(dst, window, h):
+            nc.vector.tensor_copy(dst, window[:].indirect(idx[:, 32 * h: 32 * (h + 1)]))
+
+        def v_plane(a, cols):
+            return v_s[4 * a: P, cols]
+
+        for q in range(4):
+            nc.vector.tensor_copy(out=tab_s[32 * q: 32 * q + 8, :].bitcast(I32),
+                                  in_=tab_rows[32 * q: 32 * q + 8, :].bitcast(I32))
+        gather_table(v_s[:, 0:HALF], tab_s, 0)
+        gather_table(v_s[:, HALF:S], tab_s, 1)
+        wb = deal_round(raw_a[0], False, rounded[0])
+        gather_table(v_w[0][0][:], tab_w[0], 0)
+        gather_table(v_w[0][1][:], tab_w[0], 1)
+        quantize(w1_w[0][:], w1_s[0][:], wb[:])
+        nc.vector.tensor_copy(out=w2_w[:].bitcast(U16).rearrange("p (g t q) -> p g t q", g=2, t=4),
+                              in_=w2_raw[:].bitcast(U16).rearrange("p (g q t) -> p g t q", g=2, t=4))
+        wb = deal_round(raw_a[1], False, rounded[1])
+        gather_table(v_w[1][0][:], tab_w[1], 0)
+        quantize(w1_w[1][:], w1_s[1][:], wb[:])
+
+        def silu_half(h):
+            for b in range(4):
+                cols = slice(HALF * h + P * b, HALF * h + P * (b + 1))
+                bank = psum.tile([P, HALF], F32, name="bank")
+                for t in range(4):
+                    for a in range(2):
+                        nc.tensor.matmul_mx(out=bank[:, P * t: P * (t + 1)],
+                                            lhsT=w1_w[a][:, P * t: P * (t + 1)].bitcast(E4M3),
+                                            lhsT_scale=w1_s[a][:, P * t: P * (t + 1)],
+                                            rhs=v_w[a][h][:, P * b: P * (b + 1)].bitcast(E4M3),
+                                            rhs_scale=v_plane(a, cols), start=(a == 0), stop=(a == 1))
+                dst = wide[:, 2048 * h + HALF * b: 2048 * h + HALF * (b + 1)]
+                nc.scalar.activation(dst.rearrange("p (j t) -> p j t", t=4),
+                                     bank[:].rearrange("p (t j) -> p j t", t=4), ACT.Silu)
+
+        def gain_half(h, fb, parts):
+            n = 2048 // parts
+            for i in range(parts):
+                src = wide[:, 2048 * h + n * i: 2048 * h + n * (i + 1)]
+                nc.vector.tensor_tensor(fb[:, n * i: n * (i + 1)].rearrange("p (j t) -> p j t", t=4),
+                                        src.rearrange("p (j t) -> p j t", t=4),
+                                        gain_t[:].unsqueeze(1).to_broadcast([P, n // 4, 4]), ALU.mult)
+            return fb
+
+        def h_stage(s):
+            return xs[(s // 2) % 2][:, S * (s % 2): S * (s % 2 + 1)]
+
+        def h_half(s, h):
+            g, t = divmod(s, 4)
+            cols = slice(HALF * h, HALF * (h + 1))
+            bank = psum.tile([P, HALF], F32, name="bank")
+
+            def table_pass(a):
+                nc.tensor.matmul_mx(out=bank[:], lhsT=w3_w[g][a][:, P * t: P * (t + 1)].bitcast(E4M3),
+                                    lhsT_scale=w3_s[g][a][:, P * t: P * (t + 1)],
+                                    rhs=v_w[a][h][:].bitcast(E4M3), rhs_scale=v_plane(a, cols),
+                                    start=(a == 0), stop=(a == 1))
+
+            table_pass(0)
+            nc.tensor.matmul_mx(out=bank[:], lhsT=w2_w[:, 2 * P * s: 2 * P * (s + 1)].bitcast(E2M1),
+                                lhsT_scale=w2_s[:, P * s: P * (s + 1)],
+                                rhs=f_w[h][:].bitcast(E4M3), rhs_scale=f_s[h][:], start=False, stop=False)
+            table_pass(1)
+            nc.scalar.copy(out=h_stage(s)[:, cols], in_=bank[:])
+
+        def scatter(s, j0, j1):
+            t = s % 4
+            nc.vector.tensor_tensor(pages[s][:].indirect(idx2[:, j0 // 16: j1 // 16]), h_stage(s)[:, j0:j1],
+                                    wg[t // 2][:, S * (t % 2) + j0: S * (t % 2) + j1], ALU.mult)
+
+        def after_scatter(s):
+            t = s % 4
+            nc.sync.dma_start(out=page_rows(out_1, s), in_=pages[s][:])
+            dst = pair[:].bitcast(BF16).rearrange("p (u c e) -> p u c e", u=2, e=2)[:, t // 2, :, t % 2]
+            nc.scalar.copy(out=dst, in_=pages[s][:])
+
+        def weave(c0, c1):
+            src = pair[:].rearrange("p (u c) -> p c u", u=2)[:, 1024 * c0: 1024 * c1, :]
+            nc.scalar.copy(out=wide[:, 2048 * c0: 2048 * c1].rearrange("p (c u) -> p c u", u=2), in_=src)
+
+        def plane_chunk(g, c):
+            cols = slice(1024 * c, 1024 * (c + 1))
+            quantize(pg_w[g][:, cols], pg_s[g][:, cols], wide[:, 2048 * c: 2048 * (c + 1)].bitcast(BF16))
+            nc.sync.dma_start(out=out_2[g].rearrange("p n i -> p (n i)").bitcast(I32)[:, cols],
+                              in_=pg_w[g][:, cols].bitcast(I32))
+
+        def plane_scales(g):
+            for q in range(4):
+                nc.sync.dma_start(out=out_3[g, 4 * q: 4 * q + 4, :].bitcast(I32),
+                                  in_=pg_s[g][32 * q: 32 * q + 4, :].bitcast(I32))
+
+        silu_half(0)
+        wb = deal_round(raw_b[0], True, rounded[2])
+        quantize(w3_w[0][0][:], w3_s[0][0][:], wb[:])
+        wb = deal_round(raw_b[1], False, rounded[0])
+        fb = gain_half(0, rounded[2], 4)
+        nc.vector.tensor_copy(out=w2_s[:].rearrange("p (g t q) -> p g t q", g=2, t=4),
+                              in_=w2_sraw[:].rearrange("p (g q t) -> p g t q", g=2, t=4))
+        quantize(f_w[0][:], f_s[0][:], fb[:])
+        quantize(w3_w[0][1][:], w3_s[0][1][:], wb[:])
+        h_half(0, 0)
+        v_w[1].append(held("v_w11", HALF, U32, tag="w2_sraw"))
+        gather_table(v_w[1][1][:], tab_w[1], 1)
+        silu_half(1)
+        h_half(1, 0)
+
+        for a in range(2):
+            load_rows(raw_a[1 - a], w3[512 * a: 512 * (a + 1), 512:1024])
+        load_wg(2, 4)
+        for s in range(2, 7):
+            load_page(s)
+        rain_t = [raw_b, [held(f"rain1{h}", 2048, F32, tag=f"tab_w{h}") for h in range(2)]]
+        load_rows(rain_t[0][0][:], rain[0:512, 0:HALF])
+        load_rows(rain_t[1][0][:], rain[512:1024, 0:HALF])
+        load_page(7)
+        nc.sync.dma_start(idx3[:], offs3)
+        for g in range(2):
+            load_rows(rain_t[g][1][:], rain[512 * g: 512 * (g + 1), HALF:PX])
+        for g in range(2):
+            load_words(w4_w[g], w4_words[g])
+        load_planes(w4_s, w4_scales)
+        with nc.allow_non_contiguous_dma(reason="one bias value a partition"):
+            nc.sync.dma_start(out=by_t[:], in_=by.rearrange("(c p) -> p c", p=P))
+
+        scatter(0, 0, HALF)
+        fb = gain_half(1, rounded[1], 1)
+        quantize(f_w[1][:], f_s[1][:], fb[:])
+        h_half(0, 1)
+        h_half(1, 1)
+        scatter(1, 0, HALF)
+        for a in range(2):
+            wb = deal_round(raw_a[1 - a], False, rounded[2 - 2 * a])
+            quantize(w3_w[1][a][:], w3_s[1][a][:], wb[:])
+        for s in (2, 3):
+            for h in range(2):
+                h_half(s, h)
+        scatter(0, HALF, S)
+        scatter(1, HALF, S)
+        for h in range(2):
+            h_half(4, h)
+        after_scatter(0)
+        for h in range(2):
+            h_half(5, h)
+        after_scatter(1)
+        scatter(2, 0, S)
+        for h in range(2):
+            h_half(6, h)
+        after_scatter(2)
+        scatter(3, 0, S)
+        for h in range(2):
+            h_half(7, h)
+        after_scatter(3)
+        weave(0, 2)
+        for s in range(4, 8):
+            if s == 6:
+                plane_chunk(0, 0)
+            if s == 7:
+                plane_chunk(0, 1)
+                plane_scales(0)
+            scatter(s, 0, S)
+            after_scatter(s)
+
+        pg_w.append(held("pg_w1", T2, U32, tag="wg0"))
+        y_stage = [wg[1], raw_b[0]]
+        def rain_of(g, t, j0, n):
+            h, j = divmod(j0, HALF)
+            return rain_t[g][h][:, HALF * t + j: HALF * t + j + n]
+
+        def x_gather(g, j0, n, stage, xb):
+            for t in range(4):
+                nc.vector.tensor_tensor(stage[:, n * t: n * (t + 1)],
+                                        pages[4 * g + t][:].indirect(idx3[:, j0 // 16: (j0 + n) // 16]),
+                                        rain_of(g, t, j0, n), ALU.subtract)
+            nc.scalar.copy(out=xb[:, 0: 4 * n].rearrange("p (c i t) -> p c t i", i=4, t=4),
+                           in_=stage[:, 0: 4 * n].rearrange("p (t c i) -> p c t i", i=4, t=4))
+            return xb
+
+        def x_quant(g, j0, n, xb):
+            quantize(x_w[g][:, j0: j0 + n], x_s[g][:, j0: j0 + n], xb[:, 0: 4 * n])
+
+        def y_piece(j0, n):
+            h, j = divmod(j0, HALF)
+            cols = slice(j0, j0 + n)
+            per_bank = HALF // n
+            stage = y_stage[h][:, 4 * j: 4 * (j + n)]
+            for c0 in range(0, 4, per_bank):
+                bank = psum.tile([P, HALF], F32, name="bank")
+                for c in range(c0, c0 + per_bank):
+                    for g in range(2):
+                        nc.tensor.matmul_mx(out=bank[:, n * (c - c0): n * (c - c0 + 1)],
+                                            lhsT=w4_w[g][:, P * c: P * (c + 1)].bitcast(E4M3),
+                                            lhsT_scale=w4_s[4 * g: P, P * c: P * (c + 1)],
+                                            rhs=x_w[g][:, cols].bitcast(E4M3), rhs_scale=x_s[g][:, cols],
+                                            start=(g == 0), stop=(g == 1))
+                if per_bank == 4:
+                    nc.vector.tensor_tensor(stage.rearrange("p (c j) -> p c j", c=4),
+                                            bank[:].rearrange("p (c j) -> p c j", c=4),
+                                            by_t[:].unsqueeze(2).to_broadcast([P, 4, n]), ALU.add)
+                else:
+                    for c in range(c0, c0 + per_bank):
+                        nc.scalar.activation(stage[:, n * c: n * (c + 1)], bank[:, n * (c - c0): n * (c - c0 + 1)],
+                                             ACT.Identity, bias=by_t[:, c: c + 1])
+            nc.sync.dma_start(out=out_0.rearrange("(c p) j -> p c j", p=P)[:, :, cols],
+                              in_=stage.rearrange("p (c j) -> p c j", c=4))
+
+        pieces = [(0, 0, 512), (1, 0, 512), (0, 512, 512), (1, 512, 256), (1, 768, 128), (1, 896, 128)]
+        last = None
+        for i, (g, j0, n) in enumerate(pieces):
+            if i == 0:
+                weave(0, 1)
+            xb = x_gather(g, j0, n, xs[i % 2], rounded[i % 3])
+            if i == 2:
+                weave(1, 2)
+            if last is not None:
+                x_quant(*last)
+                if last[0] == 1:
+                    y_piece(last[1], last[2])
+            if i == 1:
+                plane_chunk(1, 0)
+            if i == 3:
+                plane_chunk(1, 1)
+                plane_scales(1)
+            last = (g, j0, n, xb)
+        x_quant(*last)
+        y_piece(last[1], last[2])

@@ -35,8 +35,8 @@ def tile_list_tapping_panel_board_kernel(tc, tab_words, tab_scales, offs, offs2,
         idx3 = keep.tile([P, PX // 16], U16, name="idx3")
         tab_w = [held(f"tab_w{a}", T, U32) for a in range(2)]
         tab_s = held("tab_s", T, U8)
-        tab_rows = held("tab_rows", T, U8)
-        v_w = [[held(f"v_w{a}{h}", HALF, U32) for h in range(2 - a)] for a in range(2)]
+        tab_rows = held("tab_rows", T, U8, tag="rounded2")
+        v_w = [[held(f"v_w{a}{h}", HALF, U32) for h in range(2)] for a in range(2)]
         rounded = [held(f"rounded{i}", 2048, BF16) for i in range(3)]
         v_s = held("v_s", S, U8)
         pair = held("pair", 4096, F32)
@@ -76,9 +76,9 @@ def tile_list_tapping_panel_board_kernel(tc, tab_words, tab_scales, offs, offs2,
         def load_rows(dst, src):
             nc.sync.dma_start(out=dst.rearrange("p (j c) -> p j c", j=4), in_=src.rearrange("(p j) c -> p j c", j=4))
 
-        def load_planes(dst, src):
+        def load_planes(dst, src, quadrants=range(4)):
             passes = src.shape[0]
-            for q in range(4):
+            for q in quadrants:
                 nc.sync.dma_start(out=dst[32 * q: 32 * q + 4 * passes, :].bitcast(I32),
                                     in_=src[:, 4 * q: 4 * q + 4, :].bitcast(I32))
 
@@ -102,15 +102,15 @@ def tile_list_tapping_panel_board_kernel(tc, tab_words, tab_scales, offs, offs2,
         load_words(tab_w[0], tab_words[0])
         nc.sync.dma_start(out=w2_raw[:].bitcast(I32), in_=w2_words[0].bitcast(I32))
         load_rows(raw_a[1][:], w1[512:1024, :])
+        load_planes(w2_sraw, w2_scales, (0, 1))
         load_words(tab_w[1], tab_words[1])
-        nc.sync.dma_start(out=gain_t[:], in_=gain.rearrange("(p t) -> p t", t=4))
+        load_planes(w2_sraw, w2_scales, (2, 3))
         load_rows(raw_b[0][:], w3[0:512, 0:512])
         load_rows(raw_b[1][:], w3[512:1024, 0:512])
-        load_planes(w2_sraw, w2_scales)
-        load_wg(0, 1)
+        nc.sync.dma_start(out=gain_t[:], in_=gain.rearrange("(p t) -> p t", t=4))
+        load_wg(0, 2)
         load_page(0)
         nc.sync.dma_start(idx2[:], offs2)
-        load_wg(1, 2)
         load_page(1)
 
         def deal_round(raw, on_vector, wb):
@@ -145,6 +145,11 @@ def tile_list_tapping_panel_board_kernel(tc, tab_words, tab_scales, offs, offs2,
         wb = deal_round(raw_a[1], False, rounded[1])
         gather_table(v_w[1][0][:], tab_w[1], 0)
         quantize(w1_w[1][:], w1_s[1][:], wb[:])
+        gather_table(v_w[1][1][:], tab_w[1], 1)
+        nc.vector.tensor_copy(out=w2_s[:].rearrange("p (g t q) -> p g t q", g=2, t=4),
+                              in_=w2_sraw[:].rearrange("p (g q t) -> p g t q", g=2, t=4))
+
+        silu_out = [wide, raw_b[1]]
 
         def silu_half(h):
             for b in range(4):
@@ -157,14 +162,14 @@ def tile_list_tapping_panel_board_kernel(tc, tab_words, tab_scales, offs, offs2,
                                             lhsT_scale=w1_s[a][:, P * t: P * (t + 1)],
                                             rhs=v_w[a][h][:, P * b: P * (b + 1)].bitcast(E4M3),
                                             rhs_scale=v_plane(a, cols), start=(a == 0), stop=(a == 1))
-                dst = wide[:, 2048 * h + HALF * b: 2048 * h + HALF * (b + 1)]
+                dst = silu_out[h][:, HALF * b: HALF * (b + 1)]
                 nc.scalar.activation(dst.rearrange("p (j t) -> p j t", t=4),
                                      bank[:].rearrange("p (t j) -> p j t", t=4), ACT.Silu)
 
         def gain_half(h, fb, parts):
             n = 2048 // parts
             for i in range(parts):
-                src = wide[:, 2048 * h + n * i: 2048 * h + n * (i + 1)]
+                src = silu_out[h][:, n * i: n * (i + 1)]
                 nc.vector.tensor_tensor(fb[:, n * i: n * (i + 1)].rearrange("p (j t) -> p j t", t=4),
                                         src.rearrange("p (j t) -> p j t", t=4),
                                         gain_t[:].unsqueeze(1).to_broadcast([P, n // 4, 4]), ALU.mult)
@@ -222,15 +227,15 @@ def tile_list_tapping_panel_board_kernel(tc, tab_words, tab_scales, offs, offs2,
         quantize(w3_w[0][0][:], w3_s[0][0][:], wb[:])
         wb = deal_round(raw_b[1], False, rounded[0])
         fb = gain_half(0, rounded[2], 4)
-        nc.vector.tensor_copy(out=w2_s[:].rearrange("p (g t q) -> p g t q", g=2, t=4),
-                              in_=w2_sraw[:].rearrange("p (g q t) -> p g t q", g=2, t=4))
         quantize(f_w[0][:], f_s[0][:], fb[:])
         quantize(w3_w[0][1][:], w3_s[0][1][:], wb[:])
         h_half(0, 0)
-        v_w[1].append(held("v_w11", HALF, U32, tag="w2_sraw"))
-        gather_table(v_w[1][1][:], tab_w[1], 1)
         silu_half(1)
-        h_half(1, 0)
+        fb = gain_half(1, rounded[1], 4)
+        quantize(f_w[1][:], f_s[1][:], fb[:])
+        h_half(0, 1)
+        for h in range(2):
+            h_half(1, h)
 
         for a in range(2):
             load_rows(raw_a[1 - a], w3[512 * a: 512 * (a + 1), 512:1024])
@@ -251,11 +256,6 @@ def tile_list_tapping_panel_board_kernel(tc, tab_words, tab_scales, offs, offs2,
             nc.sync.dma_start(out=by_t[:], in_=by.rearrange("(c p) -> p c", p=P))
 
         scatter(0, 0, HALF)
-        fb = gain_half(1, rounded[1], 1)
-        quantize(f_w[1][:], f_s[1][:], fb[:])
-        h_half(0, 1)
-        h_half(1, 1)
-        scatter(1, 0, HALF)
         for a in range(2):
             wb = deal_round(raw_a[1 - a], False, rounded[2 - 2 * a])
             quantize(w3_w[1][a][:], w3_s[1][a][:], wb[:])
@@ -263,7 +263,7 @@ def tile_list_tapping_panel_board_kernel(tc, tab_words, tab_scales, offs, offs2,
             for h in range(2):
                 h_half(s, h)
         scatter(0, HALF, S)
-        scatter(1, HALF, S)
+        scatter(1, 0, S)
         for h in range(2):
             h_half(4, h)
         after_scatter(0)
@@ -290,17 +290,25 @@ def tile_list_tapping_panel_board_kernel(tc, tab_words, tab_scales, offs, offs2,
 
         pg_w.append(held("pg_w1", T2, U32, tag="wg0"))
         y_stage = [wg[1], raw_b[0]]
-        def rain_of(g, t, j0, n):
+        def rain_of(g, j0, n):
             h, j = divmod(j0, HALF)
-            return rain_t[g][h][:, HALF * t + j: HALF * t + j + n]
+            return rain_t[g][h][:].rearrange("p (t j) -> p t j", t=4)[:, :, j: j + n]
 
         def x_gather(g, j0, n, stage, xb):
+            woven = xb[:, 0: 4 * n].rearrange("p (c i t) -> p c t i", i=4, t=4)
+            picked = stage[:, 0: 4 * n].rearrange("p (t c i) -> p c t i", i=4, t=4)
             for t in range(4):
-                nc.vector.tensor_tensor(stage[:, n * t: n * (t + 1)],
-                                        pages[4 * g + t][:].indirect(idx3[:, j0 // 16: (j0 + n) // 16]),
-                                        rain_of(g, t, j0, n), ALU.subtract)
-            nc.scalar.copy(out=xb[:, 0: 4 * n].rearrange("p (c i t) -> p c t i", i=4, t=4),
-                           in_=stage[:, 0: 4 * n].rearrange("p (t c i) -> p c t i", i=4, t=4))
+                window = pages[4 * g + t][:].indirect(idx3[:, j0 // 16: (j0 + n) // 16])
+                if n >= 256:
+                    nc.vector.tensor_copy(stage[:, n * t: n * (t + 1)], window)
+                else:
+                    nc.vector.tensor_tensor(stage[:, n * t: n * (t + 1)], window, rain_of(g, j0, n)[:, t, :],
+                                            ALU.subtract)
+            if n >= 256:
+                nc.vector.tensor_tensor(woven, picked, rain_of(g, j0, n).rearrange("p t (c i) -> p c t i", i=4),
+                                        ALU.subtract)
+            else:
+                nc.scalar.copy(out=woven, in_=picked)
             return xb
 
         def x_quant(g, j0, n, xb):

@@ -299,16 +299,8 @@ def tile_list_tapping_panel_board_kernel(tc, tab_words, tab_scales, offs, offs2,
             picked = stage[:, 0: 4 * n].rearrange("p (t c i) -> p c t i", i=4, t=4)
             for t in range(4):
                 window = pages[4 * g + t][:].indirect(idx3[:, j0 // 16: (j0 + n) // 16])
-                if n >= 256:
-                    nc.vector.tensor_copy(stage[:, n * t: n * (t + 1)], window)
-                else:
-                    nc.vector.tensor_tensor(stage[:, n * t: n * (t + 1)], window, rain_of(g, j0, n)[:, t, :],
-                                            ALU.subtract)
-            if n >= 256:
-                nc.vector.tensor_tensor(woven, picked, rain_of(g, j0, n).rearrange("p t (c i) -> p c t i", i=4),
-                                        ALU.subtract)
-            else:
-                nc.scalar.copy(out=woven, in_=picked)
+                nc.vector.tensor_tensor(stage[:, n * t: n * (t + 1)], window, rain_of(g, j0, n)[:, t, :], ALU.subtract)
+            nc.scalar.copy(out=woven, in_=picked)
             return xb
 
         def x_quant(g, j0, n, xb):

@@ -15,8 +15,14 @@ E4M3 = mybir.dt.float8_e4m3fn_x4
 E2M1 = mybir.dt.float4_e2m1fn_x4
 ACT = mybir.ActivationFunctionType
 ALU = mybir.AluOpType
+
 P = 128
+PACK = 4
+PASS = P * PACK
 HALF = 512
+STAGE = PACK * HALF
+PER_COLUMN = 16
+QUADRANT = 32
 
 
 def tile_list_tapping_panel_board_kernel(tc, tab_words, tab_scales, offs, offs2, offs3, w1, gain, w2_words,
@@ -30,324 +36,311 @@ def tile_list_tapping_panel_board_kernel(tc, tab_words, tab_scales, offs, offs2,
         def held(name, cols, dtype, tag=None):
             return keep.tile([P, cols], dtype, name=name, tag=tag or name, align_bytes=64)
 
-        idx = keep.tile([P, S // 16], U16, name="idx")
-        idx2 = keep.tile([P, S // 16], U16, name="idx2")
-        idx3 = keep.tile([P, PX // 16], U16, name="idx3")
+        idx = keep.tile([P, S // PER_COLUMN], U16, name="idx")
+        idx2 = keep.tile([P, S // PER_COLUMN], U16, name="idx2")
+        idx3 = keep.tile([P, PX // PER_COLUMN], U16, name="idx3")
         tab_w = [held(f"tab_w{a}", T, U32) for a in range(2)]
         tab_s = held("tab_s", T, U8)
         tab_rows = held("tab_rows", T, U8, tag="rounded2")
-        v_w = [[held(f"v_w{a}{h}", HALF, U32) for h in range(2)] for a in range(2)]
-        rounded = [held(f"rounded{i}", 2048, BF16) for i in range(3)]
+        v_w = [[held(f"v_w{a}{half}", HALF, U32) for half in range(2)] for a in range(2)]
+        rounded = [held(f"rounded{i}", STAGE, BF16) for i in range(3)]
         v_s = held("v_s", S, U8)
-        pair = held("pair", 4096, F32)
-        raw_a = [pair[:, 2048 * a: 2048 * (a + 1)] for a in range(2)]
-        raw_b = [held(f"raw_b{a}", 2048, F32) for a in range(2)]
-        w1_w = [held(f"w1_w{a}", HALF, U32) for a in range(2)]
-        w1_s = [held(f"w1_s{a}", HALF, U8) for a in range(2)]
-        w3_w = [[held(f"w3_w{g}{a}", HALF, U32) for a in range(2)] for g in range(2)]
-        w3_s = [[held(f"w3_s{g}{a}", HALF, U8) for a in range(2)] for g in range(2)]
+        pair = held("pair", 2 * STAGE, F32)
+        raw_a = [pair[:, STAGE * i: STAGE * (i + 1)] for i in range(2)]
+        raw_b = [held(f"raw_b{i}", STAGE, F32) for i in range(2)]
+        w1_w = [held(f"w1_w{a}", M, U32) for a in range(2)]
+        w1_s = [held(f"w1_s{a}", M, U8) for a in range(2)]
+        w3_w = [[held(f"w3_w{g}{a}", PASS, U32) for a in range(2)] for g in range(2)]
+        w3_s = [[held(f"w3_s{g}{a}", PASS, U8) for a in range(2)] for g in range(2)]
         w2_raw = held("w2_raw", 2 * H, U8)
         w2_w = held("w2_w", 2 * H, U8)
         w2_sraw = held("w2_sraw", H, U8)
         w2_s = held("w2_s", H, U8)
         w4_w = [held(f"w4_w{g}", N, U32) for g in range(2)]
         w4_s = held("w4_s", N, U8)
-        wg = [held(f"wg{u}", 2 * S, F32) for u in range(2)]
+        wg = [held(f"wg{i}", 2 * S, F32) for i in range(2)]
         pages = [held(f"page{s}", T2, F32) for s in range(8)]
-        wide = held("wide", 4096, F32)
-        f_w = [held(f"f_w{h}", HALF, U32) for h in range(2)]
-        f_s = [held(f"f_s{h}", HALF, U8) for h in range(2)]
-        xs = [held(f"xs{i}", 2048, F32) for i in range(2)]
+        wide = held("wide", 2 * STAGE, F32)
+        f_w = [held(f"f_w{half}", HALF, U32) for half in range(2)]
+        f_s = [held(f"f_s{half}", HALF, U8) for half in range(2)]
+        xs = [held(f"xs{i}", STAGE, F32) for i in range(2)]
         pg_w = [held("pg_w0", T2, U32)]
         pg_s = [held(f"pg_s{g}", T2, U8) for g in range(2)]
         x_w = [held(f"x_w{g}", PX, U32) for g in range(2)]
         x_s = [held(f"x_s{g}", PX, U8) for g in range(2)]
-        gain_t = held("gain_t", 4, F32)
-        by_t = held("by_t", 4, F32)
-        warm = held("warm", 2, F32)
+        gain_t = held("gain_t", PACK, F32)
+        by_t = held("by_t", N // P, F32)
 
-        def page_rows(ap, s):
-            g, t = divmod(s, 4)
-            return ap[512 * g: 512 * (g + 1), :].rearrange("(p t) c -> p t c", t=4)[:, t, :]
+        def group_rows(ap, g):
+            return ap[PASS * g: PASS * (g + 1), :]
+
+        def slice_rows(ap, s):
+            g, t = divmod(s, PACK)
+            return group_rows(ap, g).rearrange("(p t) c -> p t c", t=PACK)[:, t, :]
+
+        def half_cols(half):
+            return slice(HALF * half, HALF * (half + 1))
+
+        def tile_cols(i):
+            return slice(P * i, P * (i + 1))
+
+        def entries(offsets, j0, j1):
+            return offsets[:, j0 // PER_COLUMN: j1 // PER_COLUMN]
 
         def load_words(dst, src):
             nc.sync.dma_start(out=dst[:].bitcast(I32), in_=src.rearrange("p n i -> p (n i)").bitcast(I32))
 
         def load_rows(dst, src):
-            nc.sync.dma_start(out=dst.rearrange("p (j c) -> p j c", j=4), in_=src.rearrange("(p j) c -> p j c", j=4))
+            nc.sync.dma_start(out=dst.rearrange("p (t c) -> p t c", t=PACK),
+                              in_=src.rearrange("(p t) c -> p t c", t=PACK))
 
-        def load_planes(dst, src, quadrants=range(4)):
+        def load_scales(dst, src, quadrants=range(4)):
             passes = src.shape[0]
             for q in quadrants:
-                nc.sync.dma_start(out=dst[32 * q: 32 * q + 4 * passes, :].bitcast(I32),
-                                    in_=src[:, 4 * q: 4 * q + 4, :].bitcast(I32))
+                nc.sync.dma_start(out=dst[QUADRANT * q: QUADRANT * q + 4 * passes, :].bitcast(I32),
+                                  in_=src[:, 4 * q: 4 * q + 4, :].bitcast(I32))
 
-        def load_wg(t0, t1):
-            rows = wgs.rearrange("(q t) j -> q (t j)", t=4)[:, t0 * S: t1 * S]
+        def load_wgs(i):
+            rows = wgs.rearrange("(p t) j -> p (t j)", t=PACK)[:, 2 * S * i: 2 * S * (i + 1)]
             for q in range(4):
-                nc.sync.dma_start(out=wg[t0 // 2][32 * q: 32 * (q + 1), (t0 % 2) * S: (t0 % 2 + t1 - t0) * S], in_=rows)
-
-        nc.vector.memset(warm[:], 0.0)
-        nc.scalar.activation(warm[:, 1:2], warm[:, 0:1], ACT.Silu)
-
-        for plane in (tab_s, w2_sraw, w4_s):
-            nc.vector.memset(plane[:].bitcast(U32), 0)
+                nc.sync.dma_start(out=wg[i][QUADRANT * q: QUADRANT * (q + 1), :], in_=rows)
 
         def load_page(s):
-            nc.sync.dma_start(out=pages[s][:], in_=page_rows(page0, s))
+            nc.sync.dma_start(out=pages[s][:], in_=slice_rows(page0, s))
+
+        for scales in (tab_s, w2_sraw, w4_s):
+            nc.vector.memset(scales[:].bitcast(U32), 0)
 
         nc.sync.dma_start(idx[:], offs)
-        load_planes(tab_rows, tab_scales)
-        load_rows(raw_a[0][:], w1[0:512, :])
+        load_scales(tab_rows, tab_scales)
+        load_rows(raw_a[0], group_rows(w1, 0))
         load_words(tab_w[0], tab_words[0])
         nc.sync.dma_start(out=w2_raw[:].bitcast(I32), in_=w2_words[0].bitcast(I32))
-        load_rows(raw_a[1][:], w1[512:1024, :])
-        load_planes(w2_sraw, w2_scales, (0, 1))
+        load_rows(raw_a[1], group_rows(w1, 1))
+        load_scales(w2_sraw, w2_scales, (0, 1))
         load_words(tab_w[1], tab_words[1])
-        load_planes(w2_sraw, w2_scales, (2, 3))
-        load_rows(raw_b[0][:], w3[0:512, 0:512])
-        load_rows(raw_b[1][:], w3[512:1024, 0:512])
-        nc.sync.dma_start(out=gain_t[:], in_=gain.rearrange("(p t) -> p t", t=4))
-        load_wg(0, 2)
+        load_scales(w2_sraw, w2_scales, (2, 3))
+        for a in range(2):
+            load_rows(raw_b[a][:], group_rows(w3, a)[:, 0:PASS])
+        nc.sync.dma_start(out=gain_t[:], in_=gain.rearrange("(p t) -> p t", t=PACK))
+        load_wgs(0)
         load_page(0)
         nc.sync.dma_start(idx2[:], offs2)
         load_page(1)
 
-        def deal_round(raw, on_vector, wb):
-            dst = wb[:].rearrange("p (t m j) -> p m j t", t=4, j=4)
-            src = raw[:].rearrange("p (j m t) -> p m j t", j=4, t=4)
-            if on_vector:
-                nc.vector.tensor_copy(out=dst, in_=src)
-            else:
-                nc.scalar.copy(out=dst, in_=src)
-            return wb
+        def deal_and_round(copy, raw, dst):
+            copy(out=dst[:].rearrange("p (t m i) -> p m i t", t=PACK, i=PACK),
+                 in_=raw.rearrange("p (i m t) -> p m i t", i=PACK, t=PACK))
 
         def quantize(words, scales, src):
             nc.vector.quantize_mx(out=words.bitcast(E4M3), scales=scales, in_=src)
 
-        def gather_table(dst, window, h):
-            nc.vector.tensor_copy(dst, window[:].indirect(idx[:, 32 * h: 32 * (h + 1)]))
+        def gather_table(dst, window, half):
+            nc.vector.tensor_copy(dst, window[:].indirect(entries(idx, HALF * half, HALF * (half + 1))))
 
-        def v_plane(a, cols):
+        def v_scales(a, cols):
             return v_s[4 * a: P, cols]
 
         for q in range(4):
-            nc.vector.tensor_copy(out=tab_s[32 * q: 32 * q + 8, :].bitcast(I32),
-                                  in_=tab_rows[32 * q: 32 * q + 8, :].bitcast(I32))
-        gather_table(v_s[:, 0:HALF], tab_s, 0)
-        gather_table(v_s[:, HALF:S], tab_s, 1)
-        wb = deal_round(raw_a[0], False, rounded[0])
-        gather_table(v_w[0][0][:], tab_w[0], 0)
-        gather_table(v_w[0][1][:], tab_w[0], 1)
-        quantize(w1_w[0][:], w1_s[0][:], wb[:])
-        nc.vector.tensor_copy(out=w2_w[:].bitcast(U16).rearrange("p (g t q) -> p g t q", g=2, t=4),
-                              in_=w2_raw[:].bitcast(U16).rearrange("p (g q t) -> p g t q", g=2, t=4))
-        wb = deal_round(raw_a[1], False, rounded[1])
+            live = slice(QUADRANT * q, QUADRANT * q + 8)
+            nc.vector.tensor_copy(out=tab_s[live, :].bitcast(I32), in_=tab_rows[live, :].bitcast(I32))
+        for half in range(2):
+            gather_table(v_s[:, half_cols(half)], tab_s, half)
+        deal_and_round(nc.scalar.copy, raw_a[0], rounded[0])
+        for half in range(2):
+            gather_table(v_w[0][half][:], tab_w[0], half)
+        quantize(w1_w[0][:], w1_s[0][:], rounded[0][:])
+        nc.vector.tensor_copy(out=w2_w[:].bitcast(U16).rearrange("p (g t m) -> p g t m", g=2, t=PACK),
+                              in_=w2_raw[:].bitcast(U16).rearrange("p (g m t) -> p g t m", g=2, t=PACK))
+        deal_and_round(nc.scalar.copy, raw_a[1], rounded[1])
         gather_table(v_w[1][0][:], tab_w[1], 0)
-        quantize(w1_w[1][:], w1_s[1][:], wb[:])
+        quantize(w1_w[1][:], w1_s[1][:], rounded[1][:])
         gather_table(v_w[1][1][:], tab_w[1], 1)
-        nc.vector.tensor_copy(out=w2_s[:].rearrange("p (g t q) -> p g t q", g=2, t=4),
-                              in_=w2_sraw[:].rearrange("p (g q t) -> p g t q", g=2, t=4))
+        nc.vector.tensor_copy(out=w2_s[:].rearrange("p (g t m) -> p g t m", g=2, t=PACK),
+                              in_=w2_sraw[:].rearrange("p (g m t) -> p g t m", g=2, t=PACK))
 
         silu_out = [wide, raw_b[1]]
 
-        def silu_half(h):
-            for b in range(4):
-                cols = slice(HALF * h + P * b, HALF * h + P * (b + 1))
+        def silu_half(half):
+            for b in range(HALF // P):
+                cols = slice(HALF * half + P * b, HALF * half + P * (b + 1))
                 bank = psum.tile([P, HALF], F32, name="bank")
-                for t in range(4):
+                for t in range(PACK):
                     for a in range(2):
-                        nc.tensor.matmul_mx(out=bank[:, P * t: P * (t + 1)],
-                                            lhsT=w1_w[a][:, P * t: P * (t + 1)].bitcast(E4M3),
-                                            lhsT_scale=w1_s[a][:, P * t: P * (t + 1)],
-                                            rhs=v_w[a][h][:, P * b: P * (b + 1)].bitcast(E4M3),
-                                            rhs_scale=v_plane(a, cols), start=(a == 0), stop=(a == 1))
-                dst = silu_out[h][:, HALF * b: HALF * (b + 1)]
-                nc.scalar.activation(dst.rearrange("p (j t) -> p j t", t=4),
-                                     bank[:].rearrange("p (t j) -> p j t", t=4), ACT.Silu)
+                        nc.tensor.matmul_mx(out=bank[:, tile_cols(t)],
+                                            lhsT=w1_w[a][:, tile_cols(t)].bitcast(E4M3),
+                                            lhsT_scale=w1_s[a][:, tile_cols(t)],
+                                            rhs=v_w[a][half][:, tile_cols(b)].bitcast(E4M3),
+                                            rhs_scale=v_scales(a, cols), start=(a == 0), stop=(a == 1))
+                nc.scalar.activation(silu_out[half][:, half_cols(b)].rearrange("p (j t) -> p j t", t=PACK),
+                                     bank[:].rearrange("p (t j) -> p j t", t=PACK), ACT.Silu)
 
-        def gain_half(h, fb, parts):
-            n = 2048 // parts
-            for i in range(parts):
-                src = silu_out[h][:, n * i: n * (i + 1)]
-                nc.vector.tensor_tensor(fb[:, n * i: n * (i + 1)].rearrange("p (j t) -> p j t", t=4),
-                                        src.rearrange("p (j t) -> p j t", t=4),
-                                        gain_t[:].unsqueeze(1).to_broadcast([P, n // 4, 4]), ALU.mult)
-            return fb
+        def gain_half(half, dst):
+            for b in range(HALF // P):
+                nc.vector.tensor_tensor(dst[:, half_cols(b)].rearrange("p (j t) -> p j t", t=PACK),
+                                        silu_out[half][:, half_cols(b)].rearrange("p (j t) -> p j t", t=PACK),
+                                        gain_t[:].unsqueeze(1).to_broadcast([P, P, PACK]), ALU.mult)
 
         def h_stage(s):
             return xs[(s // 2) % 2][:, S * (s % 2): S * (s % 2 + 1)]
 
-        def h_half(s, h):
-            g, t = divmod(s, 4)
-            cols = slice(HALF * h, HALF * (h + 1))
+        def h_half(s, half):
+            g, t = divmod(s, PACK)
             bank = psum.tile([P, HALF], F32, name="bank")
 
             def table_pass(a):
-                nc.tensor.matmul_mx(out=bank[:], lhsT=w3_w[g][a][:, P * t: P * (t + 1)].bitcast(E4M3),
-                                    lhsT_scale=w3_s[g][a][:, P * t: P * (t + 1)],
-                                    rhs=v_w[a][h][:].bitcast(E4M3), rhs_scale=v_plane(a, cols),
+                nc.tensor.matmul_mx(out=bank[:], lhsT=w3_w[g][a][:, tile_cols(t)].bitcast(E4M3),
+                                    lhsT_scale=w3_s[g][a][:, tile_cols(t)],
+                                    rhs=v_w[a][half][:].bitcast(E4M3), rhs_scale=v_scales(a, half_cols(half)),
                                     start=(a == 0), stop=(a == 1))
 
             table_pass(0)
             nc.tensor.matmul_mx(out=bank[:], lhsT=w2_w[:, 2 * P * s: 2 * P * (s + 1)].bitcast(E2M1),
-                                lhsT_scale=w2_s[:, P * s: P * (s + 1)],
-                                rhs=f_w[h][:].bitcast(E4M3), rhs_scale=f_s[h][:], start=False, stop=False)
+                                lhsT_scale=w2_s[:, tile_cols(s)],
+                                rhs=f_w[half][:].bitcast(E4M3), rhs_scale=f_s[half][:], start=False, stop=False)
             table_pass(1)
-            nc.scalar.copy(out=h_stage(s)[:, cols], in_=bank[:])
+            nc.scalar.copy(out=h_stage(s)[:, half_cols(half)], in_=bank[:])
+
+        def h_slice(s):
+            for half in range(2):
+                h_half(s, half)
 
         def scatter(s, j0, j1):
-            t = s % 4
-            nc.vector.tensor_tensor(pages[s][:].indirect(idx2[:, j0 // 16: j1 // 16]), h_stage(s)[:, j0:j1],
+            t = s % PACK
+            nc.vector.tensor_tensor(pages[s][:].indirect(entries(idx2, j0, j1)), h_stage(s)[:, j0:j1],
                                     wg[t // 2][:, S * (t % 2) + j0: S * (t % 2) + j1], ALU.mult)
 
-        def after_scatter(s):
-            t = s % 4
-            nc.sync.dma_start(out=page_rows(out_1, s), in_=pages[s][:])
-            dst = pair[:].bitcast(BF16).rearrange("p (u c e) -> p u c e", u=2, e=2)[:, t // 2, :, t % 2]
-            nc.scalar.copy(out=dst, in_=pages[s][:])
+        def store_and_round(s):
+            t = s % PACK
+            nc.sync.dma_start(out=slice_rows(out_1, s), in_=pages[s][:])
+            nc.scalar.copy(out=pair[:].bitcast(BF16).rearrange("p (u c e) -> p u c e", u=2, e=2)[:, t // 2, :, t % 2],
+                           in_=pages[s][:])
+
+        chunk = T2 // 2
 
         def weave(c0, c1):
-            src = pair[:].rearrange("p (u c) -> p c u", u=2)[:, 1024 * c0: 1024 * c1, :]
-            nc.scalar.copy(out=wide[:, 2048 * c0: 2048 * c1].rearrange("p (c u) -> p c u", u=2), in_=src)
+            src = pair[:].rearrange("p (u c) -> p c u", u=2)[:, chunk * c0: chunk * c1, :]
+            nc.scalar.copy(out=wide[:, 2 * chunk * c0: 2 * chunk * c1].rearrange("p (c u) -> p c u", u=2), in_=src)
 
-        def plane_chunk(g, c):
-            cols = slice(1024 * c, 1024 * (c + 1))
-            quantize(pg_w[g][:, cols], pg_s[g][:, cols], wide[:, 2048 * c: 2048 * (c + 1)].bitcast(BF16))
+        def quantize_page(g, c):
+            cols = slice(chunk * c, chunk * (c + 1))
+            quantize(pg_w[g][:, cols], pg_s[g][:, cols], wide[:, 2 * chunk * c: 2 * chunk * (c + 1)].bitcast(BF16))
             nc.sync.dma_start(out=out_2[g].rearrange("p n i -> p (n i)").bitcast(I32)[:, cols],
                               in_=pg_w[g][:, cols].bitcast(I32))
 
-        def plane_scales(g):
+        def store_page_scales(g):
             for q in range(4):
                 nc.sync.dma_start(out=out_3[g, 4 * q: 4 * q + 4, :].bitcast(I32),
-                                  in_=pg_s[g][32 * q: 32 * q + 4, :].bitcast(I32))
+                                  in_=pg_s[g][QUADRANT * q: QUADRANT * q + 4, :].bitcast(I32))
 
         silu_half(0)
-        wb = deal_round(raw_b[0], True, rounded[2])
-        quantize(w3_w[0][0][:], w3_s[0][0][:], wb[:])
-        wb = deal_round(raw_b[1], False, rounded[0])
-        fb = gain_half(0, rounded[2], 4)
-        quantize(f_w[0][:], f_s[0][:], fb[:])
-        quantize(w3_w[0][1][:], w3_s[0][1][:], wb[:])
+        deal_and_round(nc.vector.tensor_copy, raw_b[0][:], rounded[2])
+        quantize(w3_w[0][0][:], w3_s[0][0][:], rounded[2][:])
+        deal_and_round(nc.scalar.copy, raw_b[1][:], rounded[0])
+        gain_half(0, rounded[2])
+        quantize(f_w[0][:], f_s[0][:], rounded[2][:])
+        quantize(w3_w[0][1][:], w3_s[0][1][:], rounded[0][:])
         h_half(0, 0)
         silu_half(1)
-        fb = gain_half(1, rounded[1], 4)
-        quantize(f_w[1][:], f_s[1][:], fb[:])
+        gain_half(1, rounded[1])
+        quantize(f_w[1][:], f_s[1][:], rounded[1][:])
         h_half(0, 1)
-        for h in range(2):
-            h_half(1, h)
+        h_slice(1)
 
         for a in range(2):
-            load_rows(raw_a[1 - a], w3[512 * a: 512 * (a + 1), 512:1024])
-        load_wg(2, 4)
+            load_rows(raw_a[1 - a], group_rows(w3, a)[:, PASS:H])
+        load_wgs(1)
         for s in range(2, 7):
             load_page(s)
-        rain_t = [raw_b, [held(f"rain1{h}", 2048, F32, tag=f"tab_w{h}") for h in range(2)]]
-        load_rows(rain_t[0][0][:], rain[0:512, 0:HALF])
-        load_rows(rain_t[1][0][:], rain[512:1024, 0:HALF])
+        rain_t = [raw_b, [held(f"rain1{half}", STAGE, F32, tag=f"tab_w{half}") for half in range(2)]]
+        for g in range(2):
+            load_rows(rain_t[g][0][:], group_rows(rain, g)[:, half_cols(0)])
         load_page(7)
         nc.sync.dma_start(idx3[:], offs3)
         for g in range(2):
-            load_rows(rain_t[g][1][:], rain[512 * g: 512 * (g + 1), HALF:PX])
+            load_rows(rain_t[g][1][:], group_rows(rain, g)[:, half_cols(1)])
         for g in range(2):
             load_words(w4_w[g], w4_words[g])
-        load_planes(w4_s, w4_scales)
+        load_scales(w4_s, w4_scales)
         with nc.allow_non_contiguous_dma(reason="one bias value a partition"):
             nc.sync.dma_start(out=by_t[:], in_=by.rearrange("(c p) -> p c", p=P))
 
         scatter(0, 0, HALF)
         for a in range(2):
-            wb = deal_round(raw_a[1 - a], False, rounded[2 - 2 * a])
-            quantize(w3_w[1][a][:], w3_s[1][a][:], wb[:])
-        for s in (2, 3):
-            for h in range(2):
-                h_half(s, h)
+            deal_and_round(nc.scalar.copy, raw_a[1 - a], rounded[2 - 2 * a])
+            quantize(w3_w[1][a][:], w3_s[1][a][:], rounded[2 - 2 * a][:])
+        h_slice(2)
+        h_slice(3)
         scatter(0, HALF, S)
         scatter(1, 0, S)
-        for h in range(2):
-            h_half(4, h)
-        after_scatter(0)
-        for h in range(2):
-            h_half(5, h)
-        after_scatter(1)
-        scatter(2, 0, S)
-        for h in range(2):
-            h_half(6, h)
-        after_scatter(2)
-        scatter(3, 0, S)
-        for h in range(2):
-            h_half(7, h)
-        after_scatter(3)
+        for s in range(PACK):
+            if s >= 2:
+                scatter(s, 0, S)
+            h_slice(s + PACK)
+            store_and_round(s)
         weave(0, 2)
-        for s in range(4, 8):
-            if s == 6:
-                plane_chunk(0, 0)
-            if s == 7:
-                plane_chunk(0, 1)
-                plane_scales(0)
+        for s in range(PACK, 2 * PACK):
+            if s >= 2 * PACK - 2:
+                quantize_page(0, s - (2 * PACK - 2))
+            if s == 2 * PACK - 1:
+                store_page_scales(0)
             scatter(s, 0, S)
-            after_scatter(s)
+            store_and_round(s)
 
         pg_w.append(held("pg_w1", T2, U32, tag="wg0"))
         y_stage = [wg[1], raw_b[0]]
-        def rain_of(g, j0, n):
-            h, j = divmod(j0, HALF)
-            return rain_t[g][h][:].rearrange("p (t j) -> p t j", t=4)[:, :, j: j + n]
 
-        def x_gather(g, j0, n, stage, xb):
-            woven = xb[:, 0: 4 * n].rearrange("p (c i t) -> p c t i", i=4, t=4)
-            picked = stage[:, 0: 4 * n].rearrange("p (t c i) -> p c t i", i=4, t=4)
-            for t in range(4):
-                window = pages[4 * g + t][:].indirect(idx3[:, j0 // 16: (j0 + n) // 16])
-                nc.vector.tensor_tensor(stage[:, n * t: n * (t + 1)], window, rain_of(g, j0, n)[:, t, :], ALU.subtract)
-            nc.scalar.copy(out=woven, in_=picked)
-            return xb
-
-        def x_quant(g, j0, n, xb):
-            quantize(x_w[g][:, j0: j0 + n], x_s[g][:, j0: j0 + n], xb[:, 0: 4 * n])
+        def gather_x(g, j0, n, picked, dst):
+            half, j = divmod(j0, HALF)
+            rain_rows = rain_t[g][half][:].rearrange("p (t j) -> p t j", t=PACK)
+            for t in range(PACK):
+                nc.vector.tensor_tensor(picked[:, n * t: n * (t + 1)],
+                                        pages[PACK * g + t][:].indirect(entries(idx3, j0, j0 + n)),
+                                        rain_rows[:, t, j: j + n], ALU.subtract)
+            nc.scalar.copy(out=dst[:, 0: PACK * n].rearrange("p (c i t) -> p c t i", i=4, t=PACK),
+                           in_=picked[:, 0: PACK * n].rearrange("p (t c i) -> p c t i", i=4, t=PACK))
 
         def y_piece(j0, n):
-            h, j = divmod(j0, HALF)
+            half, j = divmod(j0, HALF)
             cols = slice(j0, j0 + n)
             per_bank = HALF // n
-            stage = y_stage[h][:, 4 * j: 4 * (j + n)]
-            for c0 in range(0, 4, per_bank):
+            stage = y_stage[half][:, (N // P) * j: (N // P) * (j + n)]
+            for c0 in range(0, N // P, per_bank):
                 bank = psum.tile([P, HALF], F32, name="bank")
                 for c in range(c0, c0 + per_bank):
                     for g in range(2):
                         nc.tensor.matmul_mx(out=bank[:, n * (c - c0): n * (c - c0 + 1)],
-                                            lhsT=w4_w[g][:, P * c: P * (c + 1)].bitcast(E4M3),
-                                            lhsT_scale=w4_s[4 * g: P, P * c: P * (c + 1)],
+                                            lhsT=w4_w[g][:, tile_cols(c)].bitcast(E4M3),
+                                            lhsT_scale=w4_s[4 * g: P, tile_cols(c)],
                                             rhs=x_w[g][:, cols].bitcast(E4M3), rhs_scale=x_s[g][:, cols],
                                             start=(g == 0), stop=(g == 1))
-                if per_bank == 4:
-                    nc.vector.tensor_tensor(stage.rearrange("p (c j) -> p c j", c=4),
-                                            bank[:].rearrange("p (c j) -> p c j", c=4),
-                                            by_t[:].unsqueeze(2).to_broadcast([P, 4, n]), ALU.add)
+                if per_bank == N // P:
+                    nc.vector.tensor_tensor(stage.rearrange("p (c j) -> p c j", j=n),
+                                            bank[:].rearrange("p (c j) -> p c j", j=n),
+                                            by_t[:].unsqueeze(2).to_broadcast([P, per_bank, n]), ALU.add)
                 else:
                     for c in range(c0, c0 + per_bank):
                         nc.scalar.activation(stage[:, n * c: n * (c + 1)], bank[:, n * (c - c0): n * (c - c0 + 1)],
                                              ACT.Identity, bias=by_t[:, c: c + 1])
             nc.sync.dma_start(out=out_0.rearrange("(c p) j -> p c j", p=P)[:, :, cols],
-                              in_=stage.rearrange("p (c j) -> p c j", c=4))
+                              in_=stage.rearrange("p (c j) -> p c j", j=n))
 
-        pieces = [(0, 0, 512), (1, 0, 512), (0, 512, 512), (1, 512, 256), (1, 768, 128), (1, 896, 128)]
-        last = None
-        for i, (g, j0, n) in enumerate(pieces):
+        def finish_x(g, j0, n, src):
+            quantize(x_w[g][:, j0: j0 + n], x_s[g][:, j0: j0 + n], src[:, 0: PACK * n])
+            if g == 1:
+                y_piece(j0, n)
+
+        pieces = [(0, 0, HALF), (1, 0, HALF), (0, HALF, HALF), (1, HALF, 256), (1, HALF + 256, P), (1, PX - P, P)]
+        for i, piece in enumerate(pieces):
             if i == 0:
                 weave(0, 1)
-            xb = x_gather(g, j0, n, xs[i % 2], rounded[i % 3])
+            gather_x(*piece, xs[i % 2], rounded[i % 3])
             if i == 2:
                 weave(1, 2)
-            if last is not None:
-                x_quant(*last)
-                if last[0] == 1:
-                    y_piece(last[1], last[2])
-            if i == 1:
-                plane_chunk(1, 0)
+            if i > 0:
+                finish_x(*pieces[i - 1], rounded[(i - 1) % 3])
+            if i in (1, 3):
+                quantize_page(1, i // 2)
             if i == 3:
-                plane_chunk(1, 1)
-                plane_scales(1)
-            last = (g, j0, n, xb)
-        x_quant(*last)
-        y_piece(last[1], last[2])
+                store_page_scales(1)
+        finish_x(*pieces[-1], rounded[(len(pieces) - 1) % 3])

from contextlib import ExitStack

import concourse.mybir as mybir

K, M, H, N, T, S, T2, PX = 1024, 512, 1024, 512, 2048, 1024, 2048, 1024
FLOPS = 2 * S * (K * M + M * H + K * H) + 2 * PX * H * N

F32 = mybir.dt.float32
BF16 = mybir.dt.bfloat16
I32 = mybir.dt.int32
U32 = mybir.dt.uint32
U16 = mybir.dt.uint16
U8 = mybir.dt.uint8
E4M3 = mybir.dt.float8_e4m3fn_x4
E2M1 = mybir.dt.float4_e2m1fn_x4
ACT = mybir.ActivationFunctionType
ALU = mybir.AluOpType

P = 128
PACK = 4
PASS = P * PACK
HALF = 512
STAGE = PACK * HALF
PER_COLUMN = 16
QUADRANT = 32


def tile_list_tapping_panel_board_kernel(tc, tab_words, tab_scales, offs, offs2, offs3, w1, gain, w2_words,
                                                  w2_scales, w3, wgs, page0, rain, w4_words, w4_scales, by,
                                                  out_0, out_1, out_2, out_3):
    nc = tc.nc
    with ExitStack() as ctx:
        keep = ctx.enter_context(tc.tile_pool(name="keep", bufs=1))
        psum = ctx.enter_context(tc.psum_pool(name="psum", bufs=8))

        def held(name, cols, dtype, tag=None):
            return keep.tile([P, cols], dtype, name=name, tag=tag or name, align_bytes=64)

        idx = keep.tile([P, S // PER_COLUMN], U16, name="idx")
        idx2 = keep.tile([P, S // PER_COLUMN], U16, name="idx2")
        idx3 = keep.tile([P, PX // PER_COLUMN], U16, name="idx3")
        tab_w = [held(f"tab_w{a}", T, U32) for a in range(2)]
        tab_s = held("tab_s", T, U8)
        tab_rows = held("tab_rows", T, U8, tag="rounded2")
        v_w = [[held(f"v_w{a}{half}", HALF, U32) for half in range(2)] for a in range(2)]
        rounded = [held(f"rounded{i}", STAGE, BF16) for i in range(3)]
        v_s = held("v_s", S, U8)
        pair = held("pair", 2 * STAGE, F32)
        raw_a = [pair[:, STAGE * i: STAGE * (i + 1)] for i in range(2)]
        raw_b = [held(f"raw_b{i}", STAGE, F32) for i in range(2)]
        w1_w = [held(f"w1_w{a}", M, U32) for a in range(2)]
        w1_s = [held(f"w1_s{a}", M, U8) for a in range(2)]
        w3_w = [[held(f"w3_w{g}{a}", PASS, U32) for a in range(2)] for g in range(2)]
        w3_s = [[held(f"w3_s{g}{a}", PASS, U8) for a in range(2)] for g in range(2)]
        w2_raw = held("w2_raw", 2 * H, U8)
        w2_w = held("w2_w", 2 * H, U8)
        w2_sraw = held("w2_sraw", H, U8)
        w2_s = held("w2_s", H, U8)
        w4_w = [held(f"w4_w{g}", N, U32) for g in range(2)]
        w4_s = held("w4_s", N, U8)
        wg = [held(f"wg{i}", 2 * S, F32) for i in range(2)]
        pages = [held(f"page{s}", T2, F32) for s in range(8)]
        wide = held("wide", 2 * STAGE, F32)
        f_w = [held(f"f_w{half}", HALF, U32) for half in range(2)]
        f_s = [held(f"f_s{half}", HALF, U8) for half in range(2)]
        xs = [held(f"xs{i}", STAGE, F32) for i in range(2)]
        pg_w = [held("pg_w0", T2, U32)]
        pg_s = [held(f"pg_s{g}", T2, U8) for g in range(2)]
        x_w = [held(f"x_w{g}", PX, U32) for g in range(2)]
        x_s = [held(f"x_s{g}", PX, U8) for g in range(2)]
        gain_t = held("gain_t", PACK, F32)
        by_t = held("by_t", N // P, F32)

        def group_rows(ap, g):
            return ap[PASS * g: PASS * (g + 1), :]

        def slice_rows(ap, s):
            g, t = divmod(s, PACK)
            return group_rows(ap, g).rearrange("(p t) c -> p t c", t=PACK)[:, t, :]

        def half_cols(half):
            return slice(HALF * half, HALF * (half + 1))

        def tile_cols(i):
            return slice(P * i, P * (i + 1))

        def entries(offsets, j0, j1):
            return offsets[:, j0 // PER_COLUMN: j1 // PER_COLUMN]

        def load_words(dst, src):
            nc.sync.dma_start(out=dst[:].bitcast(I32), in_=src.rearrange("p n i -> p (n i)").bitcast(I32))

        def load_rows(dst, src):
            nc.sync.dma_start(out=dst.rearrange("p (t c) -> p t c", t=PACK),
                              in_=src.rearrange("(p t) c -> p t c", t=PACK))

        def load_scales(dst, src, quadrants=range(4)):
            passes = src.shape[0]
            for q in quadrants:
                nc.sync.dma_start(out=dst[QUADRANT * q: QUADRANT * q + 4 * passes, :].bitcast(I32),
                                  in_=src[:, 4 * q: 4 * q + 4, :].bitcast(I32))

        def load_wgs(i):
            rows = wgs.rearrange("(p t) j -> p (t j)", t=PACK)[:, 2 * S * i: 2 * S * (i + 1)]
            for q in range(4):
                nc.sync.dma_start(out=wg[i][QUADRANT * q: QUADRANT * (q + 1), :], in_=rows)

        def load_page(s):
            nc.sync.dma_start(out=pages[s][:], in_=slice_rows(page0, s))

        for scales in (tab_s, w2_sraw, w4_s):
            nc.vector.memset(scales[:].bitcast(U32), 0)

        nc.sync.dma_start(idx[:], offs)
        load_scales(tab_rows, tab_scales)
        load_rows(raw_a[0], group_rows(w1, 0))
        load_words(tab_w[0], tab_words[0])
        nc.sync.dma_start(out=w2_raw[:].bitcast(I32), in_=w2_words[0].bitcast(I32))
        load_rows(raw_a[1], group_rows(w1, 1))
        load_scales(w2_sraw, w2_scales, (0, 1))
        load_words(tab_w[1], tab_words[1])
        load_scales(w2_sraw, w2_scales, (2, 3))
        for a in range(2):
            load_rows(raw_b[a][:], group_rows(w3, a)[:, 0:PASS])
        nc.sync.dma_start(out=gain_t[:], in_=gain.rearrange("(p t) -> p t", t=PACK))
        load_wgs(0)
        load_page(0)
        nc.sync.dma_start(idx2[:], offs2)
        load_page(1)

        def deal_and_round(copy, raw, dst):
            copy(out=dst[:].rearrange("p (t m i) -> p m i t", t=PACK, i=PACK),
                 in_=raw.rearrange("p (i m t) -> p m i t", i=PACK, t=PACK))

        def quantize(words, scales, src):
            nc.vector.quantize_mx(out=words.bitcast(E4M3), scales=scales, in_=src)

        def gather_table(dst, window, half):
            nc.vector.tensor_copy(dst, window[:].indirect(entries(idx, HALF * half, HALF * (half + 1))))

        def v_scales(a, cols):
            return v_s[4 * a: P, cols]

        for q in range(4):
            live = slice(QUADRANT * q, QUADRANT * q + 8)
            nc.vector.tensor_copy(out=tab_s[live, :].bitcast(I32), in_=tab_rows[live, :].bitcast(I32))
        for half in range(2):
            gather_table(v_s[:, half_cols(half)], tab_s, half)
        deal_and_round(nc.scalar.copy, raw_a[0], rounded[0])
        for half in range(2):
            gather_table(v_w[0][half][:], tab_w[0], half)
        quantize(w1_w[0][:], w1_s[0][:], rounded[0][:])
        nc.vector.tensor_copy(out=w2_w[:].bitcast(U16).rearrange("p (g t m) -> p g t m", g=2, t=PACK),
                              in_=w2_raw[:].bitcast(U16).rearrange("p (g m t) -> p g t m", g=2, t=PACK))
        deal_and_round(nc.scalar.copy, raw_a[1], rounded[1])
        gather_table(v_w[1][0][:], tab_w[1], 0)
        quantize(w1_w[1][:], w1_s[1][:], rounded[1][:])
        gather_table(v_w[1][1][:], tab_w[1], 1)
        nc.vector.tensor_copy(out=w2_s[:].rearrange("p (g t m) -> p g t m", g=2, t=PACK),
                              in_=w2_sraw[:].rearrange("p (g m t) -> p g t m", g=2, t=PACK))

        silu_out = [wide, raw_b[1]]

        def silu_half(half):
            for b in range(HALF // P):
                cols = slice(HALF * half + P * b, HALF * half + P * (b + 1))
                bank = psum.tile([P, HALF], F32, name="bank")
                for t in range(PACK):
                    for a in range(2):
                        nc.tensor.matmul_mx(out=bank[:, tile_cols(t)],
                                            lhsT=w1_w[a][:, tile_cols(t)].bitcast(E4M3),
                                            lhsT_scale=w1_s[a][:, tile_cols(t)],
                                            rhs=v_w[a][half][:, tile_cols(b)].bitcast(E4M3),
                                            rhs_scale=v_scales(a, cols), start=(a == 0), stop=(a == 1))
                nc.scalar.activation(silu_out[half][:, half_cols(b)].rearrange("p (j t) -> p j t", t=PACK),
                                     bank[:].rearrange("p (t j) -> p j t", t=PACK), ACT.Silu)

        def gain_half(half, dst):
            for b in range(HALF // P):
                nc.vector.tensor_tensor(dst[:, half_cols(b)].rearrange("p (j t) -> p j t", t=PACK),
                                        silu_out[half][:, half_cols(b)].rearrange("p (j t) -> p j t", t=PACK),
                                        gain_t[:].unsqueeze(1).to_broadcast([P, P, PACK]), ALU.mult)

        def h_stage(s):
            return xs[(s // 2) % 2][:, S * (s % 2): S * (s % 2 + 1)]

        def h_half(s, half):
            g, t = divmod(s, PACK)
            bank = psum.tile([P, HALF], F32, name="bank")

            def table_pass(a):
                nc.tensor.matmul_mx(out=bank[:], lhsT=w3_w[g][a][:, tile_cols(t)].bitcast(E4M3),
                                    lhsT_scale=w3_s[g][a][:, tile_cols(t)],
                                    rhs=v_w[a][half][:].bitcast(E4M3), rhs_scale=v_scales(a, half_cols(half)),
                                    start=(a == 0), stop=(a == 1))

            table_pass(0)
            nc.tensor.matmul_mx(out=bank[:], lhsT=w2_w[:, 2 * P * s: 2 * P * (s + 1)].bitcast(E2M1),
                                lhsT_scale=w2_s[:, tile_cols(s)],
                                rhs=f_w[half][:].bitcast(E4M3), rhs_scale=f_s[half][:], start=False, stop=False)
            table_pass(1)
            nc.scalar.copy(out=h_stage(s)[:, half_cols(half)], in_=bank[:])

        def h_slice(s):
            for half in range(2):
                h_half(s, half)

        def scatter(s, j0, j1):
            t = s % PACK
            nc.vector.tensor_tensor(pages[s][:].indirect(entries(idx2, j0, j1)), h_stage(s)[:, j0:j1],
                                    wg[t // 2][:, S * (t % 2) + j0: S * (t % 2) + j1], ALU.mult)

        def store_and_round(s):
            t = s % PACK
            nc.sync.dma_start(out=slice_rows(out_1, s), in_=pages[s][:])
            nc.scalar.copy(out=pair[:].bitcast(BF16).rearrange("p (u c e) -> p u c e", u=2, e=2)[:, t // 2, :, t % 2],
                           in_=pages[s][:])

        chunk = T2 // 2

        def weave(c0, c1):
            src = pair[:].rearrange("p (u c) -> p c u", u=2)[:, chunk * c0: chunk * c1, :]
            nc.scalar.copy(out=wide[:, 2 * chunk * c0: 2 * chunk * c1].rearrange("p (c u) -> p c u", u=2), in_=src)

        def quantize_page(g, c):
            cols = slice(chunk * c, chunk * (c + 1))
            quantize(pg_w[g][:, cols], pg_s[g][:, cols], wide[:, 2 * chunk * c: 2 * chunk * (c + 1)].bitcast(BF16))
            nc.sync.dma_start(out=out_2[g].rearrange("p n i -> p (n i)").bitcast(I32)[:, cols],
                              in_=pg_w[g][:, cols].bitcast(I32))

        def store_page_scales(g):
            for q in range(4):
                nc.sync.dma_start(out=out_3[g, 4 * q: 4 * q + 4, :].bitcast(I32),
                                  in_=pg_s[g][QUADRANT * q: QUADRANT * q + 4, :].bitcast(I32))

        silu_half(0)
        deal_and_round(nc.vector.tensor_copy, raw_b[0][:], rounded[2])
        quantize(w3_w[0][0][:], w3_s[0][0][:], rounded[2][:])
        deal_and_round(nc.scalar.copy, raw_b[1][:], rounded[0])
        gain_half(0, rounded[2])
        quantize(f_w[0][:], f_s[0][:], rounded[2][:])
        quantize(w3_w[0][1][:], w3_s[0][1][:], rounded[0][:])
        h_half(0, 0)
        silu_half(1)
        gain_half(1, rounded[1])
        quantize(f_w[1][:], f_s[1][:], rounded[1][:])
        h_half(0, 1)
        h_slice(1)

        for a in range(2):
            load_rows(raw_a[1 - a], group_rows(w3, a)[:, PASS:H])
        load_wgs(1)
        for s in range(2, 7):
            load_page(s)
        rain_t = [raw_b, [held(f"rain1{half}", STAGE, F32, tag=f"tab_w{half}") for half in range(2)]]
        for g in range(2):
            load_rows(rain_t[g][0][:], group_rows(rain, g)[:, half_cols(0)])
        load_page(7)
        nc.sync.dma_start(idx3[:], offs3)
        for g in range(2):
            load_rows(rain_t[g][1][:], group_rows(rain, g)[:, half_cols(1)])
        for g in range(2):
            load_words(w4_w[g], w4_words[g])
        load_scales(w4_s, w4_scales)
        with nc.allow_non_contiguous_dma(reason="one bias value a partition"):
            nc.sync.dma_start(out=by_t[:], in_=by.rearrange("(c p) -> p c", p=P))

        scatter(0, 0, HALF)
        for a in range(2):
            deal_and_round(nc.scalar.copy, raw_a[1 - a], rounded[2 - 2 * a])
            quantize(w3_w[1][a][:], w3_s[1][a][:], rounded[2 - 2 * a][:])
        h_slice(2)
        h_slice(3)
        scatter(0, HALF, S)
        scatter(1, 0, S)
        for s in range(PACK):
            if s >= 2:
                scatter(s, 0, S)
            h_slice(s + PACK)
            store_and_round(s)
        weave(0, 2)
        for s in range(PACK, 2 * PACK):
            if s >= 2 * PACK - 2:
                quantize_page(0, s - (2 * PACK - 2))
            if s == 2 * PACK - 1:
                store_page_scales(0)
            scatter(s, 0, S)
            store_and_round(s)

        pg_w.append(held("pg_w1", T2, U32, tag="wg0"))
        y_stage = [wg[1], raw_b[0]]

        def gather_x(g, j0, n, picked, dst):
            half, j = divmod(j0, HALF)
            rain_rows = rain_t[g][half][:].rearrange("p (t j) -> p t j", t=PACK)
            for t in range(PACK):
                nc.vector.tensor_tensor(picked[:, n * t: n * (t + 1)],
                                        pages[PACK * g + t][:].indirect(entries(idx3, j0, j0 + n)),
                                        rain_rows[:, t, j: j + n], ALU.subtract)
            nc.scalar.copy(out=dst[:, 0: PACK * n].rearrange("p (c i t) -> p c t i", i=4, t=PACK),
                           in_=picked[:, 0: PACK * n].rearrange("p (t c i) -> p c t i", i=4, t=PACK))

        def y_piece(j0, n):
            half, j = divmod(j0, HALF)
            cols = slice(j0, j0 + n)
            per_bank = HALF // n
            stage = y_stage[half][:, (N // P) * j: (N // P) * (j + n)]
            for c0 in range(0, N // P, per_bank):
                bank = psum.tile([P, HALF], F32, name="bank")
                for c in range(c0, c0 + per_bank):
                    for g in range(2):
                        nc.tensor.matmul_mx(out=bank[:, n * (c - c0): n * (c - c0 + 1)],
                                            lhsT=w4_w[g][:, tile_cols(c)].bitcast(E4M3),
                                            lhsT_scale=w4_s[4 * g: P, tile_cols(c)],
                                            rhs=x_w[g][:, cols].bitcast(E4M3), rhs_scale=x_s[g][:, cols],
                                            start=(g == 0), stop=(g == 1))
                if per_bank == N // P:
                    nc.vector.tensor_tensor(stage.rearrange("p (c j) -> p c j", j=n),
                                            bank[:].rearrange("p (c j) -> p c j", j=n),
                                            by_t[:].unsqueeze(2).to_broadcast([P, per_bank, n]), ALU.add)
                else:
                    for c in range(c0, c0 + per_bank):
                        nc.scalar.activation(stage[:, n * c: n * (c + 1)], bank[:, n * (c - c0): n * (c - c0 + 1)],
                                             ACT.Identity, bias=by_t[:, c: c + 1])
            nc.sync.dma_start(out=out_0.rearrange("(c p) j -> p c j", p=P)[:, :, cols],
                              in_=stage.rearrange("p (c j) -> p c j", j=n))

        def finish_x(g, j0, n, src):
            quantize(x_w[g][:, j0: j0 + n], x_s[g][:, j0: j0 + n], src[:, 0: PACK * n])
            if g == 1:
                y_piece(j0, n)

        pieces = [(0, 0, HALF), (1, 0, HALF), (0, HALF, HALF), (1, HALF, 256), (1, HALF + 256, P), (1, PX - P, P)]
        for i, piece in enumerate(pieces):
            if i == 0:
                weave(0, 1)
            gather_x(*piece, xs[i % 2], rounded[i % 3])
            if i == 2:
                weave(1, 2)
            if i > 0:
                finish_x(*pieces[i - 1], rounded[(i - 1) % 3])
            if i in (1, 3):
                quantize_page(1, i // 2)
            if i == 3:
                store_page_scales(1)
        finish_x(*pieces[-1], rounded[(len(pieces) - 1) % 3])
